import numpy as np
import ml_dtypes


def mxq(x, axis, fmt="e4m3"):
    dtype, down = {"e4m3": (ml_dtypes.float8_e4m3fn, 7), "e5m2": (ml_dtypes.float8_e5m2, 14)}[fmt]
    v = np.moveaxis(np.asarray(x, np.float32).astype(ml_dtypes.bfloat16).astype(np.float64), axis, -1)
    blocks = v.reshape(v.shape[:-1] + (-1, 32))
    amax = np.abs(blocks).max(-1, keepdims=True)
    byte = np.maximum(np.where(amax > 0, np.frexp(amax)[1] - 1 + 127, 0) - down, 1)
    scale = np.exp2(byte - 127.0)
    codes = (blocks / scale).astype(np.float32).astype(dtype).astype(np.float64)
    return np.moveaxis((codes * scale).reshape(v.shape), -1, axis)


WIDE = False


def mx_kscale(k, group=512):
    if not WIDE:
        return np.ones(k)
    levels = np.array([18, -18])
    if group != 512:
        return np.exp2(np.random.permutation(np.resize(levels, k // group))).repeat(group)
    if k % 512:
        return np.exp2(np.random.permutation(np.resize(levels, k // 32))).repeat(32)
    a = np.empty((k // 512, 16))
    for p in range(k // 512):
        a[p, :8] = np.random.permutation(np.resize(levels, 8))
        for g in range(8):
            far = levels[np.abs(levels - a[p, g]) >= 10]
            a[p, g + 8] = far[np.random.randint(len(far))]
    return np.exp2(a.ravel()).repeat(32)


def f64(x):
    return np.asarray(x).astype(np.float64)


def silu(v):
    return v / (1.0 + np.exp(-v))


K, R, M, N = 512, 128, 1024, 512


def setup_inputs():
    n = np.random.standard_normal
    s = mx_kscale(K)[:, None]
    z = mx_kscale(R, 0)
    return {
        "x": (n((K, N)) * s).astype(np.float32),
        "w": (n((K, M)) / np.sqrt(K) / s).astype(np.float32),
        "a": (n((K, R)) / np.sqrt(K) / s * z).astype(np.float32),
        "bb": (n((R, M)) / np.sqrt(R) / z[:, None]).astype(np.float32),
        "b": (0.5 * n((M, 1))).astype(np.float32),
    }


def reference(x, w, a, bb, b):
    xq = mxq(f64(x), 0, "e4m3")
    z = mxq(f64(a), 0, "e4m3").T @ xq
    y = (mxq(f64(w), 0, "e4m3").T @ xq) + (mxq(f64(bb), 0, "e4m3").T @ mxq(z, 0, "e4m3"))
    y = y + f64(b)
    y = silu(y)
    return y

@@ -1,0 +1,240 @@
+from contextlib import ExitStack
+
+import concourse.mybir as mybir
+
+K, R, M, N = 512, 128, 1024, 512
+FLOPS = 2 * (K * R * N + K * M * N + R * M * N)
+
+F32 = mybir.dt.float32
+BF16 = mybir.dt.bfloat16
+I32 = mybir.dt.int32
+U32 = mybir.dt.uint32
+U8 = mybir.dt.uint8
+FP8X4 = mybir.dt.float8_e4m3fn_x4
+SILU = mybir.ActivationFunctionType.Silu
+ADD = mybir.AluOpType.add
+
+P = 128
+PACK = 4
+ROWS = 32
+TILES = P // ROWS
+NQ = 128
+QUARTERS = N // NQ
+M_TILES = M // P
+W_STEP = 256
+
+
+def interleave(copy, dst, src):
+    copy(
+        out=dst.rearrange("p (c i t) -> p c t i", i=4, t=PACK),
+        in_=src.rearrange("p t (c i) -> p c t i", i=4),
+    )
+
+
+def tile_rows_lora_silu_bias_kernel(tc, x, w, a, bb, b, out):
+    nc = tc.nc
+    with ExitStack() as ctx:
+        sb = ctx.enter_context(tc.tile_pool(name="sb", bufs=1))
+        ps = ctx.enter_context(tc.psum_pool(name="ps", bufs=1))
+        ctx.enter_context(tc.manual_schedule())
+
+        def tiles(name, count, width, dtype):
+            return [sb.tile([P, width], dtype, name="%s%d" % (name, i), align_bytes=64) for i in range(count)]
+
+        def operand(name, count, columns):
+            return (
+                tiles(name + "_bf", count, PACK * columns, BF16),
+                tiles(name + "_codes", count, columns, U32),
+                tiles(name + "_scales", count, columns, U8),
+            )
+
+        def quantize(op, i):
+            nc.vector.quantize_mx(out=op[1][i][:].bitcast(FP8X4), scales=op[2][i][:], in_=op[0][i][:])
+
+        full_banks = [ps.tile([P, N], F32, name="full%d" % i) for i in range(4)]
+        row_banks = [ps.tile([P, N], F32, name="row%d" % i) for i in range(TILES)]
+
+        a_raw = sb.tile([P, PACK, R], F32, name="a_raw")
+        x_raw = sb.tile([P, PACK, N], F32, name="x_raw")
+        bb_raw = sb.tile([P, PACK, W_STEP], F32, name="bb_raw")
+        w_loads = [(0, 256), (256, 768), (768, 1024)]
+        w_raw = [sb.tile([P, PACK, hi - lo], F32, name="w_raw%d" % lo) for lo, hi in w_loads]
+
+        a_op = operand("a", 1, R)
+        a4_codes = sb.tile([P, PACK * P], U32, name="a4_codes", align_bytes=64)
+        a4_scales = sb.tile([P, PACK * P], U8, name="a4_scales", align_bytes=64)
+        x_op = operand("x", QUARTERS, NQ)
+        z_op = operand("z", QUARTERS, NQ)
+        bb_op = operand("bb", 1, W_STEP)
+        w_op = operand("w", M // W_STEP, W_STEP)
+        lora = tiles("lora", M_TILES, N, F32)
+        y = tiles("y", M_TILES, N, F32)
+        res = tiles("res", M_TILES, N, F32)
+        bias_rows = sb.tile([P, ROWS], F32, name="bias_rows", align_bytes=64)
+        bias = sb.tile([P, ROWS], F32, name="bias", align_bytes=64)
+        warm_in = sb.tile([P, 1], F32, name="warm_in")
+        warm_out = sb.tile([P, 1], F32, name="warm_out")
+
+        nc.sync.dma_start(out=a_raw[:], in_=a.rearrange("(p j) r -> p j r", j=PACK))
+        nc.sync.dma_start(out=x_raw[:], in_=x.rearrange("(p j) n -> p j n", j=PACK))
+        for g in (0, 2, 1, 3):
+            nc.sync.dma_start(
+                out=bb_raw[ROWS * g : ROWS * (g + 1)],
+                in_=bb[:, W_STEP * g : W_STEP * (g + 1)].rearrange("(p j) m -> p j m", j=PACK),
+            )
+        for i, (lo, hi) in enumerate(w_loads):
+            nc.sync.dma_start(out=w_raw[i][:], in_=w[:, lo:hi].rearrange("(p j) m -> p j m", j=PACK))
+
+        nc.gpsimd.memset(bias_rows[:], 0.0)
+        b_rows = b.rearrange("(t q e) o -> q t (e o)", q=TILES, e=ROWS)
+        for q in range(TILES):
+            nc.gpsimd.dma_start(out=bias_rows[ROWS * q : ROWS * q + M_TILES, :], in_=b_rows[q])
+
+        nc.vector.memset(warm_in[:], 0.0)
+        nc.scalar.activation(out=warm_out[:], in_=warm_in[:], func=SILU)
+        nc.vector.memset(a_op[2][0][:].bitcast(I32), 0)
+
+        nc.vector.tensor_copy(
+            out=a_op[0][0][:].rearrange("p (j e k) -> p e k j", j=PACK, k=PACK),
+            in_=a_raw[:].rearrange("p k (e j) -> p e k j", j=PACK),
+        )
+        quantize(a_op, 0)
+        for src, dst in ((a_op[1][0], a4_codes), (a_op[2][0], a4_scales)):
+            words = src[:].bitcast(I32).rearrange("p (j e) -> p j e", j=PACK)
+            nc.vector.tensor_copy(
+                out=dst[:].bitcast(I32).rearrange("p (j g e) -> p j g e", j=PACK, g=TILES),
+                in_=words.unsqueeze(2).to_broadcast([P, PACK, TILES, words.shape[2]]),
+            )
+
+        def x_round(copy, q):
+            interleave(copy, x_op[0][q][:], x_raw[:, :, NQ * q : NQ * (q + 1)])
+
+        def z_product(q):
+            for j in range(PACK):
+                cols = slice(P * j, P * (j + 1))
+                nc.tensor.matmul_mx(
+                    out=full_banks[q][:, NQ * j : NQ * (j + 1)],
+                    lhsT=a4_codes[:, cols].bitcast(FP8X4),
+                    lhsT_scale=a4_scales[:, cols],
+                    rhs=x_op[1][q][:].bitcast(FP8X4),
+                    rhs_scale=x_op[2][q][:],
+                    start=True,
+                    stop=True,
+                )
+
+        def z_round(q):
+            nc.scalar.copy(
+                out=z_op[0][q][:].rearrange("p (n j) -> p n j", j=PACK),
+                in_=full_banks[q][:].rearrange("p (j n) -> p n j", j=PACK),
+            )
+
+        def w_round(s):
+            i = [k for k, (lo, hi) in enumerate(w_loads) if lo <= W_STEP * s < hi][0]
+            lo = W_STEP * s - w_loads[i][0]
+            interleave(nc.vector.tensor_copy, w_op[0][s][:], w_raw[i][:, :, lo : lo + W_STEP])
+
+        def lora_product(t, q):
+            g, h = divmod(t, 2)
+            rows = slice(ROWS * g, ROWS * (g + 1))
+            cols = slice(P * h, P * (h + 1))
+            nc.tensor.matmul_mx(
+                out=row_banks[g][:, NQ * q : NQ * (q + 1)],
+                lhsT=bb_op[1][0][rows, cols].bitcast(FP8X4),
+                lhsT_scale=bb_op[2][0][rows, cols],
+                rhs=z_op[1][q][rows, :].bitcast(FP8X4),
+                rhs_scale=z_op[2][q][rows, :],
+                start=True,
+                stop=True,
+            )
+
+        def lora_tile(t):
+            for q in range(QUARTERS):
+                lora_product(t, q)
+
+        def main_tile(t):
+            s, h = divmod(t, 2)
+            cols = slice(P * h, P * (h + 1))
+            for q in range(QUARTERS):
+                nc.tensor.matmul_mx(
+                    out=full_banks[t % 4][:, NQ * q : NQ * (q + 1)],
+                    lhsT=w_op[1][s][:, cols].bitcast(FP8X4),
+                    lhsT_scale=w_op[2][s][:, cols],
+                    rhs=x_op[1][q][:].bitcast(FP8X4),
+                    rhs_scale=x_op[2][q][:],
+                    start=True,
+                    stop=True,
+                )
+
+        def lora_out(copy, t):
+            copy(out=lora[t][:], in_=row_banks[t // 2][:])
+
+        def add(t):
+            nc.vector.tensor_tensor(out=y[t][:], in0=full_banks[t % 4][:], in1=lora[t][:], op=ADD)
+
+        def finish(t):
+            nc.scalar.activation(out=res[t][:], in_=y[t][:], func=SILU, bias=bias[:, t : t + 1])
+            nc.sync.dma_start(out=out[P * t : P * (t + 1), :], in_=res[t][:])
+
+        x_round(nc.vector.tensor_copy, 0)
+        x_round(nc.scalar.copy, 2)
+        x_round(nc.vector.tensor_copy, 1)
+        x_round(nc.scalar.copy, 3)
+        for q in range(QUARTERS):
+            quantize(x_op, q)
+            z_product(q)
+        z_round(0)
+        z_round(1)
+        interleave(nc.vector.tensor_copy, bb_op[0][0][:], bb_raw[:])
+        quantize(z_op, 0)
+        quantize(bb_op, 0)
+        quantize(z_op, 1)
+        z_round(2)
+        z_round(3)
+        w_round(0)
+        quantize(z_op, 2)
+        quantize(z_op, 3)
+        quantize(w_op, 0)
+        nc.vector.transpose(out=bias[:], in_=bias_rows[:])
+        for q in range(QUARTERS):
+            for g in range(TILES):
+                lora_product(2 * g, q)
+        main_tile(0)
+        main_tile(1)
+
+        lora_out(nc.scalar.copy, 0)
+        lora_out(nc.vector.tensor_copy, 2)
+        lora_out(nc.scalar.copy, 4)
+        lora_tile(1)
+        lora_tile(3)
+        add(0)
+        lora_out(nc.scalar.copy, 1)
+        w_round(1)
+        finish(0)
+        add(1)
+        lora_tile(5)
+        quantize(w_op, 1)
+        main_tile(2)
+        main_tile(3)
+        lora_out(nc.scalar.copy, 3)
+        w_round(2)
+        finish(1)
+        add(2)
+        lora_out(nc.scalar.copy, 6)
+        lora_tile(7)
+        quantize(w_op, 2)
+        main_tile(4)
+        main_tile(5)
+        finish(2)
+        add(3)
+        lora_out(nc.scalar.copy, 5)
+        w_round(3)
+        finish(3)
+        add(4)
+        lora_out(nc.scalar.copy, 7)
+        quantize(w_op, 3)
+        main_tile(6)
+        main_tile(7)
+        finish(4)
+        for t in (5, 6, 7):
+            add(t)
+            finish(t)

@@ -12,22 +12,23 @@ U32 = mybir.dt.uint32
 U8 = mybir.dt.uint8
 FP8X4 = mybir.dt.float8_e4m3fn_x4
 SILU = mybir.ActivationFunctionType.Silu
-ADD = mybir.AluOpType.add
 
 P = 128
 PACK = 4
-ROWS = 32
-TILES = P // ROWS
-NQ = 128
-QUARTERS = N // NQ
-M_TILES = M // P
-W_STEP = 256
+ROWS = R // PACK
+ROW_TILES = P // ROWS
+N_PASS = 128
+QUARTERS = N // N_PASS
+OUT_TILES = M // P
+CHUNK = M // ROW_TILES
+FULL_BANKS = 4
+LINE = 4
 
 
-def interleave(copy, dst, src):
+def round_and_interleave(copy, dst, src):
     copy(
-        out=dst.rearrange("p (c i t) -> p c t i", i=4, t=PACK),
-        in_=src.rearrange("p t (c i) -> p c t i", i=4),
+        out=dst.rearrange("p (c i j) -> p c j i", i=LINE, j=PACK),
+        in_=src.rearrange("p j (c i) -> p c j i", i=LINE),
     )
 
 
@@ -38,203 +39,182 @@ def tile_rows_lora_silu_bias_kernel(tc, x, w, a, bb, b, out):
         ps = ctx.enter_context(tc.psum_pool(name="ps", bufs=1))
         ctx.enter_context(tc.manual_schedule())
 
-        def tiles(name, count, width, dtype):
-            return [sb.tile([P, width], dtype, name="%s%d" % (name, i), align_bytes=64) for i in range(count)]
+        def tile(name, width, dtype):
+            return sb.tile([P, width], dtype, name=name, align_bytes=64)
 
-        def operand(name, count, columns):
-            return (
-                tiles(name + "_bf", count, PACK * columns, BF16),
-                tiles(name + "_codes", count, columns, U32),
-                tiles(name + "_scales", count, columns, U8),
-            )
+        def operand(name, columns):
+            return {
+                "bf16": tile(name + "_bf16", PACK * columns, BF16),
+                "codes": tile(name + "_codes", columns, U32),
+                "scales": tile(name + "_scales", columns, U8),
+            }
 
-        def quantize(op, i):
-            nc.vector.quantize_mx(out=op[1][i][:].bitcast(FP8X4), scales=op[2][i][:], in_=op[0][i][:])
+        def quantize(op):
+            nc.vector.quantize_mx(out=op["codes"][:].bitcast(FP8X4), scales=op["scales"][:], in_=op["bf16"][:])
 
-        full_banks = [ps.tile([P, N], F32, name="full%d" % i) for i in range(4)]
-        row_banks = [ps.tile([P, N], F32, name="row%d" % i) for i in range(TILES)]
-
-        a_raw = sb.tile([P, PACK, R], F32, name="a_raw")
-        x_raw = sb.tile([P, PACK, N], F32, name="x_raw")
-        bb_raw = sb.tile([P, PACK, W_STEP], F32, name="bb_raw")
-        w_loads = [(0, 256), (256, 768), (768, 1024)]
-        w_raw = [sb.tile([P, PACK, hi - lo], F32, name="w_raw%d" % lo) for lo, hi in w_loads]
-
-        a_op = operand("a", 1, R)
-        a4_codes = sb.tile([P, PACK * P], U32, name="a4_codes", align_bytes=64)
-        a4_scales = sb.tile([P, PACK * P], U8, name="a4_scales", align_bytes=64)
-        x_op = operand("x", QUARTERS, NQ)
-        z_op = operand("z", QUARTERS, NQ)
-        bb_op = operand("bb", 1, W_STEP)
-        w_op = operand("w", M // W_STEP, W_STEP)
-        lora = tiles("lora", M_TILES, N, F32)
-        y = tiles("y", M_TILES, N, F32)
-        res = tiles("res", M_TILES, N, F32)
-        bias_rows = sb.tile([P, ROWS], F32, name="bias_rows", align_bytes=64)
-        bias = sb.tile([P, ROWS], F32, name="bias", align_bytes=64)
-        warm_in = sb.tile([P, 1], F32, name="warm_in")
-        warm_out = sb.tile([P, 1], F32, name="warm_out")
-
-        nc.sync.dma_start(out=a_raw[:], in_=a.rearrange("(p j) r -> p j r", j=PACK))
-        nc.sync.dma_start(out=x_raw[:], in_=x.rearrange("(p j) n -> p j n", j=PACK))
-        for g in (0, 2, 1, 3):
-            nc.sync.dma_start(
-                out=bb_raw[ROWS * g : ROWS * (g + 1)],
-                in_=bb[:, W_STEP * g : W_STEP * (g + 1)].rearrange("(p j) m -> p j m", j=PACK),
-            )
-        for i, (lo, hi) in enumerate(w_loads):
-            nc.sync.dma_start(out=w_raw[i][:], in_=w[:, lo:hi].rearrange("(p j) m -> p j m", j=PACK))
-
-        nc.gpsimd.memset(bias_rows[:], 0.0)
-        b_rows = b.rearrange("(t q e) o -> q t (e o)", q=TILES, e=ROWS)
-        for q in range(TILES):
-            nc.gpsimd.dma_start(out=bias_rows[ROWS * q : ROWS * q + M_TILES, :], in_=b_rows[q])
-
-        nc.vector.memset(warm_in[:], 0.0)
-        nc.scalar.activation(out=warm_out[:], in_=warm_in[:], func=SILU)
-        nc.vector.memset(a_op[2][0][:].bitcast(I32), 0)
-
-        nc.vector.tensor_copy(
-            out=a_op[0][0][:].rearrange("p (j e k) -> p e k j", j=PACK, k=PACK),
-            in_=a_raw[:].rearrange("p k (e j) -> p e k j", j=PACK),
-        )
-        quantize(a_op, 0)
-        for src, dst in ((a_op[1][0], a4_codes), (a_op[2][0], a4_scales)):
-            words = src[:].bitcast(I32).rearrange("p (j e) -> p j e", j=PACK)
-            nc.vector.tensor_copy(
-                out=dst[:].bitcast(I32).rearrange("p (j g e) -> p j g e", j=PACK, g=TILES),
-                in_=words.unsqueeze(2).to_broadcast([P, PACK, TILES, words.shape[2]]),
-            )
-
-        def x_round(copy, q):
-            interleave(copy, x_op[0][q][:], x_raw[:, :, NQ * q : NQ * (q + 1)])
-
-        def z_product(q):
-            for j in range(PACK):
-                cols = slice(P * j, P * (j + 1))
-                nc.tensor.matmul_mx(
-                    out=full_banks[q][:, NQ * j : NQ * (j + 1)],
-                    lhsT=a4_codes[:, cols].bitcast(FP8X4),
-                    lhsT_scale=a4_scales[:, cols],
-                    rhs=x_op[1][q][:].bitcast(FP8X4),
-                    rhs_scale=x_op[2][q][:],
-                    start=True,
-                    stop=True,
-                )
-
-        def z_round(q):
-            nc.scalar.copy(
-                out=z_op[0][q][:].rearrange("p (n j) -> p n j", j=PACK),
-                in_=full_banks[q][:].rearrange("p (j n) -> p n j", j=PACK),
-            )
-
-        def w_round(s):
-            i = [k for k, (lo, hi) in enumerate(w_loads) if lo <= W_STEP * s < hi][0]
-            lo = W_STEP * s - w_loads[i][0]
-            interleave(nc.vector.tensor_copy, w_op[0][s][:], w_raw[i][:, :, lo : lo + W_STEP])
-
-        def lora_product(t, q):
-            g, h = divmod(t, 2)
-            rows = slice(ROWS * g, ROWS * (g + 1))
-            cols = slice(P * h, P * (h + 1))
+        def product(acc, stationary, cols, moving, rows):
             nc.tensor.matmul_mx(
-                out=row_banks[g][:, NQ * q : NQ * (q + 1)],
-                lhsT=bb_op[1][0][rows, cols].bitcast(FP8X4),
-                lhsT_scale=bb_op[2][0][rows, cols],
-                rhs=z_op[1][q][rows, :].bitcast(FP8X4),
-                rhs_scale=z_op[2][q][rows, :],
+                out=acc,
+                lhsT=stationary["codes"][rows, cols].bitcast(FP8X4),
+                lhsT_scale=stationary["scales"][rows, cols],
+                rhs=moving["codes"][rows, :].bitcast(FP8X4),
+                rhs_scale=moving["scales"][rows, :],
                 start=True,
                 stop=True,
             )
 
-        def lora_tile(t):
+        def part(i, width):
+            return slice(width * i, width * (i + 1))
+
+        def rows_of_four(dram):
+            return dram.rearrange("(p j) c -> p j c", j=PACK)
+
+        all_rows = slice(0, P)
+        full_banks = [ps.tile([P, N], F32, name="full%d" % i) for i in range(FULL_BANKS)]
+        row_banks = [ps.tile([P, N], F32, name="row%d" % g) for g in range(ROW_TILES)]
+
+        a_raw = sb.tile([P, PACK, R], F32, name="a_raw")
+        x_raw = sb.tile([P, PACK, N], F32, name="x_raw")
+        bb_raw = sb.tile([P, PACK, CHUNK], F32, name="bb_raw")
+        w_raw = [sb.tile([P, PACK, CHUNK], F32, name="w_raw%d" % s) for s in range(M // CHUNK)]
+        zero = tile("zero", 1, F32)
+        bias_rows = tile("bias_rows", OUT_TILES * ROWS, F32)
+        bias = tile("bias", OUT_TILES * ROWS, F32)
+
+        a_op = operand("a", R)
+        a_wide = {"codes": tile("a_wide_codes", PACK * P, U32), "scales": tile("a_wide_scales", PACK * P, U8)}
+        x_ops = [operand("x%d" % q, N_PASS) for q in range(QUARTERS)]
+        z_ops = [operand("z%d" % q, N_PASS) for q in range(QUARTERS)]
+        bb_ops = [operand("bb%d" % half, P) for half in range(2)]
+        w_ops = [operand("w%d" % s, CHUNK) for s in range(M // CHUNK)]
+        first_sum = [tile("first_sum%d" % t, N, F32) for t in range(OUT_TILES)]
+        both_sums = [tile("both_sums%d" % t, N, F32) for t in range(OUT_TILES)]
+        result = [tile("result%d" % t, N, F32) for t in range(OUT_TILES)]
+
+        nc.sync.dma_start(out=a_raw[:], in_=rows_of_four(a))
+        nc.sync.dma_start(out=x_raw[:], in_=rows_of_four(x))
+        nc.gpsimd.memset(zero[:], 0.0)
+        nc.scalar.activation(out=bias_rows[:], in_=zero[:].to_broadcast([P, OUT_TILES * ROWS]), func=SILU)
+        nc.sync.dma_start(
+            out=bias_rows[0:P:ROWS, :].rearrange("q (t e) -> q t e", e=ROWS),
+            in_=b.rearrange("(t q e) o -> q t (e o)", q=ROW_TILES, e=ROWS),
+        )
+        nc.sync.dma_start(out=w_raw[0][:], in_=rows_of_four(w[:, part(0, CHUNK)]))
+        for g in (0, 2, 1, 3):
+            nc.sync.dma_start(out=bb_raw[part(g, ROWS)], in_=rows_of_four(bb[:, part(g, CHUNK)]))
+        for s in range(1, M // CHUNK):
+            nc.sync.dma_start(out=w_raw[s][:], in_=rows_of_four(w[:, part(s, CHUNK)]))
+
+        nc.vector.memset(a_op["scales"][:].bitcast(I32), 0)
+        nc.vector.tensor_copy(
+            out=a_op["bf16"][:].rearrange("p (j e k) -> p e j k", j=PACK, k=PACK),
+            in_=a_raw[:].rearrange("p k (e j) -> p e j k", j=PACK),
+        )
+        quantize(a_op)
+        for key in ("codes", "scales"):
+            words = a_op[key][:].bitcast(I32).rearrange("p (j e) -> p j e", j=PACK)
+            nc.vector.tensor_copy(
+                out=a_wide[key][:].bitcast(I32).rearrange("p (j g e) -> p j g e", j=PACK, g=ROW_TILES),
+                in_=words.unsqueeze(2).to_broadcast([P, PACK, ROW_TILES, words.shape[2]]),
+            )
+
+        def round_w(s):
+            round_and_interleave(nc.vector.tensor_copy, w_ops[s]["bf16"][:], w_raw[s][:])
+
+        def main_product(t):
+            s, half = divmod(t, 2)
             for q in range(QUARTERS):
-                lora_product(t, q)
+                product(full_banks[t % FULL_BANKS][:, part(q, N_PASS)], w_ops[s], part(half, P), x_ops[q], all_rows)
 
-        def main_tile(t):
-            s, h = divmod(t, 2)
-            cols = slice(P * h, P * (h + 1))
+        def round_bb(half):
+            round_and_interleave(nc.vector.tensor_copy, bb_ops[half]["bf16"][:], bb_raw[:, :, part(half, P)])
+
+        def rank_product(t):
+            g, half = divmod(t, 2)
             for q in range(QUARTERS):
-                nc.tensor.matmul_mx(
-                    out=full_banks[t % 4][:, NQ * q : NQ * (q + 1)],
-                    lhsT=w_op[1][s][:, cols].bitcast(FP8X4),
-                    lhsT_scale=w_op[2][s][:, cols],
-                    rhs=x_op[1][q][:].bitcast(FP8X4),
-                    rhs_scale=x_op[2][q][:],
-                    start=True,
-                    stop=True,
-                )
+                product(row_banks[g][:, part(q, N_PASS)], bb_ops[half], slice(0, P), z_ops[q], part(g, ROWS))
 
-        def lora_out(copy, t):
-            copy(out=lora[t][:], in_=row_banks[t // 2][:])
+        def copy_rank_sum(copy, t):
+            copy(out=first_sum[t][:], in_=row_banks[t // 2][:])
+            if t % 2 == 0:
+                rank_product(t + 1)
 
-        def add(t):
-            nc.vector.tensor_tensor(out=y[t][:], in0=full_banks[t % 4][:], in1=lora[t][:], op=ADD)
+        def add_sums(t, cols):
+            bank = row_banks[0] if t < 2 else full_banks[t % FULL_BANKS]
+            nc.vector.tensor_tensor(
+                out=both_sums[t][:, cols], in0=bank[:, cols], in1=first_sum[t][:, cols], op=mybir.AluOpType.add
+            )
 
-        def finish(t):
-            nc.scalar.activation(out=res[t][:], in_=y[t][:], func=SILU, bias=bias[:, t : t + 1])
-            nc.sync.dma_start(out=out[P * t : P * (t + 1), :], in_=res[t][:])
+        def silu_and_store(t, cols):
+            nc.scalar.activation(
+                out=result[t][:, cols],
+                in_=both_sums[t][:, cols],
+                func=SILU,
+                bias=bias[:, ROWS * t : ROWS * t + 1],
+            )
+            nc.sync.dma_start(out=out[part(t, P), cols], in_=result[t][:, cols])
 
-        x_round(nc.vector.tensor_copy, 0)
-        x_round(nc.scalar.copy, 2)
-        x_round(nc.vector.tensor_copy, 1)
-        x_round(nc.scalar.copy, 3)
         for q in range(QUARTERS):
-            quantize(x_op, q)
-            z_product(q)
-        z_round(0)
-        z_round(1)
-        interleave(nc.vector.tensor_copy, bb_op[0][0][:], bb_raw[:])
-        quantize(z_op, 0)
-        quantize(bb_op, 0)
-        quantize(z_op, 1)
-        z_round(2)
-        z_round(3)
-        w_round(0)
-        quantize(z_op, 2)
-        quantize(z_op, 3)
-        quantize(w_op, 0)
+            copy = nc.vector.tensor_copy if q < QUARTERS // 2 else nc.scalar.copy
+            round_and_interleave(copy, x_ops[q]["bf16"][:], x_raw[:, :, part(q, N_PASS)])
+        for q in range(QUARTERS):
+            quantize(x_ops[q])
+            for j in range(PACK):
+                product(full_banks[q][:, part(j, N_PASS)], a_wide, part(j, P), x_ops[q], all_rows)
+            nc.scalar.copy(
+                out=z_ops[q]["bf16"][:].rearrange("p (n j) -> p n j", j=PACK),
+                in_=full_banks[q][:].rearrange("p (j n) -> p n j", j=PACK),
+            )
+
+        round_w(0)
+        quantize(z_ops[0])
+        quantize(w_ops[0])
+        quantize(z_ops[1])
+        for t in (0, 1):
+            main_product(t)
+            nc.scalar.copy(out=first_sum[t][:], in_=full_banks[t][:])
         nc.vector.transpose(out=bias[:], in_=bias_rows[:])
-        for q in range(QUARTERS):
-            for g in range(TILES):
-                lora_product(2 * g, q)
-        main_tile(0)
-        main_tile(1)
+        quantize(z_ops[2])
+        round_bb(0)
+        quantize(z_ops[3])
+        quantize(bb_ops[0])
+        for g in range(ROW_TILES):
+            rank_product(2 * g)
+        round_bb(1)
 
-        lora_out(nc.scalar.copy, 0)
-        lora_out(nc.vector.tensor_copy, 2)
-        lora_out(nc.scalar.copy, 4)
-        lora_tile(1)
-        lora_tile(3)
-        add(0)
-        lora_out(nc.scalar.copy, 1)
-        w_round(1)
-        finish(0)
-        add(1)
-        lora_tile(5)
-        quantize(w_op, 1)
-        main_tile(2)
-        main_tile(3)
-        lora_out(nc.scalar.copy, 3)
-        w_round(2)
-        finish(1)
-        add(2)
-        lora_out(nc.scalar.copy, 6)
-        lora_tile(7)
-        quantize(w_op, 2)
-        main_tile(4)
-        main_tile(5)
-        finish(2)
-        add(3)
-        lora_out(nc.scalar.copy, 5)
-        w_round(3)
-        finish(3)
-        add(4)
-        lora_out(nc.scalar.copy, 7)
-        quantize(w_op, 3)
-        main_tile(6)
-        main_tile(7)
-        finish(4)
-        for t in (5, 6, 7):
-            add(t)
-            finish(t)
+        whole = slice(0, N)
+        round_w(1)
+        quantize(bb_ops[1])
+        copy_rank_sum(nc.scalar.copy, 2)
+        copy_rank_sum(nc.scalar.copy, 4)
+        add_sums(0, whole)
+        rank_product(1)
+        quantize(w_ops[1])
+        main_product(2)
+        main_product(3)
+        silu_and_store(0, whole)
+        copy_rank_sum(nc.vector.tensor_copy, 6)
+        copy_rank_sum(nc.scalar.copy, 3)
+        round_w(2)
+        add_sums(1, whole)
+        copy_rank_sum(nc.scalar.copy, 5)
+        quantize(w_ops[2])
+        main_product(4)
+        main_product(5)
+        silu_and_store(1, whole)
+        copy_rank_sum(nc.scalar.copy, 7)
+        round_w(3)
+        add_sums(2, whole)
+        quantize(w_ops[3])
+        main_product(6)
+        silu_and_store(2, whole)
+        add_sums(3, whole)
+        main_product(7)
+        silu_and_store(3, whole)
+        for t in (4, 5, 6):
+            add_sums(t, whole)
+            silu_and_store(t, whole)
+        for half in range(2):
+            add_sums(7, part(half, N // 2))
+        for half in range(2):
+            silu_and_store(7, part(half, N // 2))

from contextlib import ExitStack

import concourse.mybir as mybir

K, R, M, N = 512, 128, 1024, 512
FLOPS = 2 * (K * R * N + K * M * N + R * M * N)

F32 = mybir.dt.float32
BF16 = mybir.dt.bfloat16
I32 = mybir.dt.int32
U32 = mybir.dt.uint32
U8 = mybir.dt.uint8
FP8X4 = mybir.dt.float8_e4m3fn_x4
SILU = mybir.ActivationFunctionType.Silu

P = 128
PACK = 4
ROWS = R // PACK
ROW_TILES = P // ROWS
N_PASS = 128
QUARTERS = N // N_PASS
OUT_TILES = M // P
CHUNK = M // ROW_TILES
FULL_BANKS = 4
LINE = 4


def round_and_interleave(copy, dst, src):
    copy(
        out=dst.rearrange("p (c i j) -> p c j i", i=LINE, j=PACK),
        in_=src.rearrange("p j (c i) -> p c j i", i=LINE),
    )


def tile_rows_lora_silu_bias_kernel(tc, x, w, a, bb, b, out):
    nc = tc.nc
    with ExitStack() as ctx:
        sb = ctx.enter_context(tc.tile_pool(name="sb", bufs=1))
        ps = ctx.enter_context(tc.psum_pool(name="ps", bufs=1))
        ctx.enter_context(tc.manual_schedule())

        def tile(name, width, dtype):
            return sb.tile([P, width], dtype, name=name, align_bytes=64)

        def operand(name, columns):
            return {
                "bf16": tile(name + "_bf16", PACK * columns, BF16),
                "codes": tile(name + "_codes", columns, U32),
                "scales": tile(name + "_scales", columns, U8),
            }

        def quantize(op):
            nc.vector.quantize_mx(out=op["codes"][:].bitcast(FP8X4), scales=op["scales"][:], in_=op["bf16"][:])

        def product(acc, stationary, cols, moving, rows):
            nc.tensor.matmul_mx(
                out=acc,
                lhsT=stationary["codes"][rows, cols].bitcast(FP8X4),
                lhsT_scale=stationary["scales"][rows, cols],
                rhs=moving["codes"][rows, :].bitcast(FP8X4),
                rhs_scale=moving["scales"][rows, :],
                start=True,
                stop=True,
            )

        def part(i, width):
            return slice(width * i, width * (i + 1))

        def rows_of_four(dram):
            return dram.rearrange("(p j) c -> p j c", j=PACK)

        all_rows = slice(0, P)
        full_banks = [ps.tile([P, N], F32, name="full%d" % i) for i in range(FULL_BANKS)]
        row_banks = [ps.tile([P, N], F32, name="row%d" % g) for g in range(ROW_TILES)]

        a_raw = sb.tile([P, PACK, R], F32, name="a_raw")
        x_raw = sb.tile([P, PACK, N], F32, name="x_raw")
        bb_raw = sb.tile([P, PACK, CHUNK], F32, name="bb_raw")
        w_raw = [sb.tile([P, PACK, CHUNK], F32, name="w_raw%d" % s) for s in range(M // CHUNK)]
        zero = tile("zero", 1, F32)
        bias_rows = tile("bias_rows", OUT_TILES * ROWS, F32)
        bias = tile("bias", OUT_TILES * ROWS, F32)

        a_op = operand("a", R)
        a_wide = {"codes": tile("a_wide_codes", PACK * P, U32), "scales": tile("a_wide_scales", PACK * P, U8)}
        x_ops = [operand("x%d" % q, N_PASS) for q in range(QUARTERS)]
        z_ops = [operand("z%d" % q, N_PASS) for q in range(QUARTERS)]
        bb_ops = [operand("bb%d" % half, P) for half in range(2)]
        w_ops = [operand("w%d" % s, CHUNK) for s in range(M // CHUNK)]
        first_sum = [tile("first_sum%d" % t, N, F32) for t in range(OUT_TILES)]
        both_sums = [tile("both_sums%d" % t, N, F32) for t in range(OUT_TILES)]
        result = [tile("result%d" % t, N, F32) for t in range(OUT_TILES)]

        nc.sync.dma_start(out=a_raw[:], in_=rows_of_four(a))
        nc.sync.dma_start(out=x_raw[:], in_=rows_of_four(x))
        nc.gpsimd.memset(zero[:], 0.0)
        nc.scalar.activation(out=bias_rows[:], in_=zero[:].to_broadcast([P, OUT_TILES * ROWS]), func=SILU)
        nc.sync.dma_start(
            out=bias_rows[0:P:ROWS, :].rearrange("q (t e) -> q t e", e=ROWS),
            in_=b.rearrange("(t q e) o -> q t (e o)", q=ROW_TILES, e=ROWS),
        )
        nc.sync.dma_start(out=w_raw[0][:], in_=rows_of_four(w[:, part(0, CHUNK)]))
        for g in (0, 2, 1, 3):
            nc.sync.dma_start(out=bb_raw[part(g, ROWS)], in_=rows_of_four(bb[:, part(g, CHUNK)]))
        for s in range(1, M // CHUNK):
            nc.sync.dma_start(out=w_raw[s][:], in_=rows_of_four(w[:, part(s, CHUNK)]))

        nc.vector.memset(a_op["scales"][:].bitcast(I32), 0)
        nc.vector.tensor_copy(
            out=a_op["bf16"][:].rearrange("p (j e k) -> p e j k", j=PACK, k=PACK),
            in_=a_raw[:].rearrange("p k (e j) -> p e j k", j=PACK),
        )
        quantize(a_op)
        for key in ("codes", "scales"):
            words = a_op[key][:].bitcast(I32).rearrange("p (j e) -> p j e", j=PACK)
            nc.vector.tensor_copy(
                out=a_wide[key][:].bitcast(I32).rearrange("p (j g e) -> p j g e", j=PACK, g=ROW_TILES),
                in_=words.unsqueeze(2).to_broadcast([P, PACK, ROW_TILES, words.shape[2]]),
            )

        def round_w(s):
            round_and_interleave(nc.vector.tensor_copy, w_ops[s]["bf16"][:], w_raw[s][:])

        def main_product(t):
            s, half = divmod(t, 2)
            for q in range(QUARTERS):
                product(full_banks[t % FULL_BANKS][:, part(q, N_PASS)], w_ops[s], part(half, P), x_ops[q], all_rows)

        def round_bb(half):
            round_and_interleave(nc.vector.tensor_copy, bb_ops[half]["bf16"][:], bb_raw[:, :, part(half, P)])

        def rank_product(t):
            g, half = divmod(t, 2)
            for q in range(QUARTERS):
                product(row_banks[g][:, part(q, N_PASS)], bb_ops[half], slice(0, P), z_ops[q], part(g, ROWS))

        def copy_rank_sum(copy, t):
            copy(out=first_sum[t][:], in_=row_banks[t // 2][:])
            if t % 2 == 0:
                rank_product(t + 1)

        def add_sums(t, cols):
            bank = row_banks[0] if t < 2 else full_banks[t % FULL_BANKS]
            nc.vector.tensor_tensor(
                out=both_sums[t][:, cols], in0=bank[:, cols], in1=first_sum[t][:, cols], op=mybir.AluOpType.add
            )

        def silu_and_store(t, cols):
            nc.scalar.activation(
                out=result[t][:, cols],
                in_=both_sums[t][:, cols],
                func=SILU,
                bias=bias[:, ROWS * t : ROWS * t + 1],
            )
            nc.sync.dma_start(out=out[part(t, P), cols], in_=result[t][:, cols])

        for q in range(QUARTERS):
            copy = nc.vector.tensor_copy if q < QUARTERS // 2 else nc.scalar.copy
            round_and_interleave(copy, x_ops[q]["bf16"][:], x_raw[:, :, part(q, N_PASS)])
        for q in range(QUARTERS):
            quantize(x_ops[q])
            for j in range(PACK):
                product(full_banks[q][:, part(j, N_PASS)], a_wide, part(j, P), x_ops[q], all_rows)
            nc.scalar.copy(
                out=z_ops[q]["bf16"][:].rearrange("p (n j) -> p n j", j=PACK),
                in_=full_banks[q][:].rearrange("p (j n) -> p n j", j=PACK),
            )

        round_w(0)
        quantize(z_ops[0])
        quantize(w_ops[0])
        quantize(z_ops[1])
        for t in (0, 1):
            main_product(t)
            nc.scalar.copy(out=first_sum[t][:], in_=full_banks[t][:])
        nc.vector.transpose(out=bias[:], in_=bias_rows[:])
        quantize(z_ops[2])
        round_bb(0)
        quantize(z_ops[3])
        quantize(bb_ops[0])
        for g in range(ROW_TILES):
            rank_product(2 * g)
        round_bb(1)

        whole = slice(0, N)
        round_w(1)
        quantize(bb_ops[1])
        copy_rank_sum(nc.scalar.copy, 2)
        copy_rank_sum(nc.scalar.copy, 4)
        add_sums(0, whole)
        rank_product(1)
        quantize(w_ops[1])
        main_product(2)
        main_product(3)
        silu_and_store(0, whole)
        copy_rank_sum(nc.vector.tensor_copy, 6)
        copy_rank_sum(nc.scalar.copy, 3)
        round_w(2)
        add_sums(1, whole)
        copy_rank_sum(nc.scalar.copy, 5)
        quantize(w_ops[2])
        main_product(4)
        main_product(5)
        silu_and_store(1, whole)
        copy_rank_sum(nc.scalar.copy, 7)
        round_w(3)
        add_sums(2, whole)
        quantize(w_ops[3])
        main_product(6)
        silu_and_store(2, whole)
        add_sums(3, whole)
        main_product(7)
        silu_and_store(3, whole)
        for t in (4, 5, 6):
            add_sums(t, whole)
            silu_and_store(t, whole)
        for half in range(2):
            add_sums(7, part(half, N // 2))
        for half in range(2):
            silu_and_store(7, part(half, N // 2))
